import numpy as np
import ml_dtypes


def mxq(x, axis, fmt="e4m3"):
    dtype, down = {"e4m3": (ml_dtypes.float8_e4m3fn, 7), "e5m2": (ml_dtypes.float8_e5m2, 14)}[fmt]
    v = np.moveaxis(np.asarray(x, np.float32).astype(ml_dtypes.bfloat16).astype(np.float64), axis, -1)
    blocks = v.reshape(v.shape[:-1] + (-1, 32))
    amax = np.abs(blocks).max(-1, keepdims=True)
    byte = np.maximum(np.where(amax > 0, np.frexp(amax)[1] - 1 + 127, 0) - down, 1)
    scale = np.exp2(byte - 127.0)
    codes = (blocks / scale).astype(np.float32).astype(dtype).astype(np.float64)
    return np.moveaxis((codes * scale).reshape(v.shape), -1, axis)


WIDE = False


def mx_kscale(k):
    if not WIDE:
        return np.ones(k)
    levels = np.array([10, -10, 5, -5, 0])
    if k % 512:
        return np.exp2(np.random.permutation(np.resize(levels, k // 32))).repeat(32)
    a = np.empty((k // 512, 16))
    for p in range(k // 512):
        a[p, :8] = np.random.permutation(np.resize(levels, 8))
        for g in range(8):
            far = levels[np.abs(levels - a[p, g]) >= 10]
            a[p, g + 8] = far[np.random.randint(len(far))]
    return np.exp2(a.ravel()).repeat(32)


def f64(x):
    return np.asarray(x).astype(np.float64)


def striped(idx):
    return np.tile(idx.reshape(-1, 16).T, (8, 1)).astype(np.uint16)


def unstriped(offs):
    return offs[:16].T.reshape(-1).astype(np.int64)


def pack_weight(w):
    k, n = w.shape
    w = f64(np.asarray(w, np.float32).astype(ml_dtypes.bfloat16)).reshape(k // 32, 32, n)
    amax = np.abs(w).max(1)
    byte = np.clip(np.where(amax > 0, np.frexp(amax)[1] - 1 + 127 - 7, 1), 1, 254)
    scaled = (w * np.exp2(127.0 - byte)[:, None, :]).reshape(k, n).astype(np.float32)
    words = np.ascontiguousarray(scaled.reshape(k // 512, 128, 4, n).transpose(0, 1, 3, 2)).astype(ml_dtypes.float8_e4m3fn).view(np.uint8)
    return words, np.ascontiguousarray(byte.astype(np.uint8).reshape(k // 512, 16, n))


def unpack_weight(words, scales):
    g, p, n, _ = words.shape
    vals = np.ascontiguousarray(words).view(ml_dtypes.float8_e4m3fn).astype(np.float64) * np.repeat(np.exp2(scales.astype(np.float64) - 127.0), 8, axis=1)[..., None]
    return vals.transpose(0, 1, 3, 2).reshape(g * 512, n)


def silu(v):
    return v / (1.0 + np.exp(-np.maximum(v, -700.0)))


K, T, S, D, H, N = 1024, 1024, 512, 4, 512, 128


def setup_inputs():
    n = np.random.standard_normal
    s = mx_kscale(K)[:, None]
    u = mx_kscale(H)
    packed_w2 = pack_weight(n((H, N)) / np.sqrt(H) / u[:, None])
    return {
        "xT": (n((K, T)) * s).astype(np.float32),
        "w1": (n((K, H)) / np.sqrt(K) / s * u).astype(np.float32),
        "w2_words": packed_w2[0],
        "w2_scales": packed_w2[1],
        "taps": (n((H, D)) / np.sqrt(D)).astype(np.float32),
        "offs": striped(np.random.permutation(T)[:S]),
    }


def reference(xT, w1, w2_words, w2_scales, taps, offs):
    xq = mxq(f64(xT)[:, unstriped(offs)], 0, "e4m3")
    h = mxq(f64(w1), 0, "e4m3").T @ xq
    z = silu(f64(taps)[:, 0:1] * h + f64(taps)[:, 1:2] * (np.pad(h, ((0, 0), (1, 0)))[:, :S]) + f64(taps)[:, 2:3] * (np.pad(h, ((0, 0), (2, 0)))[:, :S]) + f64(taps)[:, 3:4] * (np.pad(h, ((0, 0), (3, 0)))[:, :S]))
    return unpack_weight(w2_words, w2_scales).T @ mxq(z, 0, "e4m3")

@@ -1,0 +1,218 @@
+from contextlib import ExitStack
+
+import concourse.mybir as mybir
+
+K, T, S, D, H, N = 1024, 1024, 512, 4, 512, 128
+FLOPS = 2 * K * H * S + 2 * H * N * S
+
+F32 = mybir.dt.float32
+BF16 = mybir.dt.bfloat16
+I32 = mybir.dt.int32
+U32 = mybir.dt.uint32
+U16 = mybir.dt.uint16
+U8 = mybir.dt.uint8
+FP8X4 = mybir.dt.float8_e4m3fn_x4
+COPY = mybir.ActivationFunctionType.Copy
+SILU = mybir.ActivationFunctionType.Silu
+MULT = mybir.AluOpType.mult
+ADD = mybir.AluOpType.add
+
+P = 128
+PACK = 4
+K_PASS = P * PACK
+PASSES = K // K_PASS
+
+X_CHUNKS = [(0, 0, 512, 128), (0, 512, 512, 128), (1, 0, 512, 128), (1, 512, 256, 64), (1, 768, 256, 160)]
+W_CHUNKS = [(0, 0, 64, 0), (0, 64, 64, 0), (1, 0, 64, 16), (1, 64, 64, 44)]
+SPANS = [(0, 384), (384, 128)]
+
+
+def tile_picked_dconv_silu_e_kernel(tc, xT, w1, w2_words, w2_scales, taps, offs, out):
+    nc = tc.nc
+    with ExitStack() as ctx:
+        keep = ctx.enter_context(tc.tile_pool(name="keep", bufs=1))
+        psum = ctx.enter_context(tc.psum_pool(name="psum", bufs=1))
+
+        zero_in = keep.tile([P, 1], F32, name="zero_in")
+        zero_bias = keep.tile([P, 1], F32, name="zero_bias")
+        nc.vector.memset(zero_in[:], 0.0)
+        nc.scalar.activation(zero_bias[:], zero_in[:], SILU)
+
+        x_scales = keep.tile([P, T], U8, name="x_scales", align_bytes=64)
+        w2_plane = keep.tile([P, N], U8, name="w2_plane", align_bytes=64)
+        nc.vector.memset(x_scales[:].bitcast(I32), 0)
+        nc.vector.memset(w2_plane[:].bitcast(I32), 0)
+
+        offsets = keep.tile([P, S // 16], U16, name="offsets")
+        taps_sb = keep.tile([P, PACK, D], F32, name="taps_sb")
+        x_raw = []
+        for c, (g, n0, n, nv) in enumerate(X_CHUNKS):
+            raw = keep.tile([P, PACK, n], F32, name=f"x_raw{c}")
+            nc.sync.dma_start(out=raw[:], in_=xT[g * K_PASS : (g + 1) * K_PASS, n0 : n0 + n].rearrange("(p j) n -> p j n", j=PACK))
+            x_raw.append(raw)
+            if c == 0:
+                nc.sync.dma_start(offsets[:], offs)
+        nc.sync.dma_start(out=taps_sb[:], in_=taps.rearrange("(p t) d -> p t d", t=PACK))
+        w_raw = []
+        for c, (g, m0, m, mv) in enumerate(W_CHUNKS):
+            raw = keep.tile([P, PACK, PACK * m], F32, name=f"w_raw{c}")
+            nc.sync.dma_start(
+                out=raw[:],
+                in_=w1[g * K_PASS : (g + 1) * K_PASS, PACK * m0 : PACK * (m0 + m)].rearrange("(p j) n -> p j n", j=PACK),
+            )
+            w_raw.append(raw)
+        w2_codes = keep.tile([P, N], U32, name="w2_codes", align_bytes=64)
+        nc.sync.dma_start(out=w2_codes[:].bitcast(I32), in_=w2_words[0].rearrange("p n r -> p (n r)").bitcast(I32))
+        for q in range(4):
+            nc.sync.dma_start(
+                out=w2_plane[32 * q : 32 * q + 4, :].bitcast(I32), in_=w2_scales[0, 4 * q : 4 * q + 4, :].bitcast(I32)
+            )
+
+        x_words = [keep.tile([P, T], U32, name=f"x_words{g}", align_bytes=64) for g in range(PASSES)]
+        picked_words = [keep.tile([P, S], U32, name=f"picked_words{g}", align_bytes=64) for g in range(PASSES)]
+        picked_scales = keep.tile([P, S], U8, name="picked_scales", align_bytes=64)
+        for c, (g, n0, n, nv) in enumerate(X_CHUNKS):
+            grouped = keep.tile([P, n, PACK], BF16, name=f"x_grouped{c}", align_bytes=64)
+            ns = n - nv
+            dst = grouped[:].rearrange("p (c i) j -> p c j i", i=4)
+            src = x_raw[c][:].rearrange("p j (c i) -> p c j i", i=4)
+            nc.scalar.activation(dst[:, 0 : ns // 4], src[:, 0 : ns // 4], COPY)
+            nc.vector.tensor_copy(dst[:, ns // 4 :], src[:, ns // 4 :])
+            nc.vector.quantize_mx(
+                out=x_words[g][:, n0 : n0 + n].bitcast(FP8X4),
+                scales=x_scales[4 * g :, n0 : n0 + n],
+                in_=grouped[:].rearrange("p n j -> p (n j)"),
+            )
+            if n0 + n == T:
+                if g == PASSES - 1:
+                    nc.vector.tensor_copy(picked_scales[:], x_scales[:].indirect(offsets[:]))
+                nc.vector.tensor_copy(picked_words[g][:], x_words[g][:].indirect(offsets[:]))
+
+        w_grouped = [keep.tile([P, PACK, P, PACK], BF16, name=f"w_grouped{g}", align_bytes=64) for g in range(PASSES)]
+        w_words = [keep.tile([P, H], U32, name=f"w_words{g}", align_bytes=64) for g in range(PASSES)]
+        w_scales = [keep.tile([P, H], U8, name=f"w_scales{g}", align_bytes=64) for g in range(PASSES)]
+        banks = [psum.tile([P, S], F32, name=f"h_bank{t}") for t in range(PACK)]
+
+        def first_product(g, t):
+            cols = slice(t * P, (t + 1) * P)
+            nc.tensor.matmul_mx(
+                out=banks[t][:],
+                lhsT=w_words[g][:, cols].bitcast(FP8X4),
+                lhsT_scale=w_scales[g][:, cols],
+                rhs=picked_words[g][:].bitcast(FP8X4),
+                rhs_scale=picked_scales[4 * g :, :],
+                start=(g == 0),
+                stop=(g == PASSES - 1),
+            )
+
+        for c, (g, m0, m, mv) in enumerate(W_CHUNKS):
+            ms = m - mv
+            dst = w_grouped[g][:, :, m0 : m0 + m, :].rearrange("p t m j -> p m j t")
+            src = w_raw[c][:].rearrange("p j (m t) -> p m j t", t=PACK)
+            nc.scalar.activation(dst[:, 0:ms], src[:, 0:ms], COPY)
+            if mv:
+                nc.vector.tensor_copy(dst[:, ms:], src[:, ms:])
+            if m0 + m == P:
+                if g == 0:
+                    nc.vector.quantize_mx(
+                        out=w_words[g][:].bitcast(FP8X4),
+                        scales=w_scales[g][:],
+                        in_=w_grouped[g][:].rearrange("p t m j -> p (t m j)"),
+                    )
+                    first_product(0, 0)
+                    first_product(0, 1)
+                    first_product(0, 2)
+                else:
+                    for t in range(PACK):
+                        cols = slice(t * P, (t + 1) * P)
+                        nc.vector.quantize_mx(
+                            out=w_words[g][:, cols].bitcast(FP8X4),
+                            scales=w_scales[g][:, cols],
+                            in_=w_grouped[g][:, t].rearrange("p m j -> p (m j)"),
+                        )
+
+        conv = [keep.tile([P, PACK, n], F32, name=f"conv{s}") for s, (n0, n) in enumerate(SPANS)]
+
+        def tap_zero(s, t):
+            n0, n = SPANS[s]
+            if t == 0:
+                nc.vector.tensor_scalar(conv[s][:, t, :], banks[t][:, n0 : n0 + n], taps_sb[:, t, 0:1], None, MULT)
+            else:
+                nc.scalar.activation(conv[s][:, t, :], banks[t][:, n0 : n0 + n], COPY, scale=taps_sb[:, t, 0:1])
+
+        def tap_add(s, t, d):
+            n0, n = SPANS[s]
+            skip = max(d - n0, 0)
+            nc.vector.scalar_tensor_tensor(
+                out=conv[s][:, t, skip:],
+                in0=banks[t][:, n0 + skip - d : n0 + n - d],
+                scalar=taps_sb[:, t, d : d + 1],
+                in1=conv[s][:, t, skip:],
+                op0=MULT,
+                op1=ADD,
+            )
+
+        for t in range(PACK):
+            if t >= 3:
+                first_product(0, t)
+            first_product(1, t)
+            tap_zero(0, t)
+            tap_zero(1, t)
+
+        order = [(0, 0, 1), (1, 0, 1), (0, 0, 2), (1, 0, 2), (0, 1, 1), (0, 0, 3), (0, 1, 2), (0, 2, 1), (0, 1, 3),
+                 (0, 2, 2), (0, 3, 1), (0, 2, 3), (0, 3, 2), (1, 0, 3), (0, 3, 3)]
+        for s, t, d in order:
+            tap_add(s, t, d)
+
+        z_grouped = [keep.tile([P, n, PACK], BF16, name=f"z_grouped{s}", align_bytes=64) for s, (n0, n) in enumerate(SPANS)]
+        z_words = keep.tile([P, S], U32, name="z_words", align_bytes=64)
+        z_scales = keep.tile([P, S], U8, name="z_scales", align_bytes=64)
+        out_banks = [psum.tile([P, n], F32, name=f"out_bank{s}") for s, (n0, n) in enumerate(SPANS)]
+        staged = [keep.tile([P, n], F32, name=f"staged{s}") for s, (n0, n) in enumerate(SPANS)]
+
+        def activate(s, a, n):
+            nc.scalar.activation(
+                z_grouped[s][:, a : a + n, :].rearrange("p (c i) t -> p c t i", i=4),
+                conv[s][:, :, a : a + n].rearrange("p t (c i) -> p c t i", i=4),
+                SILU,
+                bias=zero_bias[:],
+            )
+
+        def second_product(s, a, n):
+            n0 = SPANS[s][0]
+            cols = slice(n0 + a, n0 + a + n)
+            nc.vector.quantize_mx(
+                out=z_words[:, cols].bitcast(FP8X4),
+                scales=z_scales[:, cols],
+                in_=z_grouped[s][:, a : a + n, :].rearrange("p n t -> p (n t)"),
+            )
+            nc.tensor.matmul_mx(
+                out=out_banks[s][:, a : a + n],
+                lhsT=w2_codes[:].bitcast(FP8X4),
+                lhsT_scale=w2_plane[:],
+                rhs=z_words[:, cols].bitcast(FP8X4),
+                rhs_scale=z_scales[:, cols],
+                start=True,
+                stop=True,
+            )
+
+        def store(s):
+            n0, n = SPANS[s]
+            if s == 0:
+                nc.scalar.copy(staged[s][:], out_banks[s][:])
+            else:
+                nc.vector.tensor_copy(staged[s][:], out_banks[s][:])
+            nc.sync.dma_start(out=out[:, n0 : n0 + n], in_=staged[s][:])
+
+        activate(0, 0, 256)
+        activate(0, 256, 128)
+        for d in range(1, D):
+            for t in range(1, PACK):
+                tap_add(1, t, d)
+            if d == 2:
+                second_product(0, 0, 256)
+        activate(1, 0, 128)
+        second_product(0, 256, 128)
+        store(0)
+        second_product(1, 0, 128)
+        store(1)

@@ -22,8 +22,8 @@ PACK = 4
 K_PASS = P * PACK
 PASSES = K // K_PASS
 
-X_CHUNKS = [(0, 0, 512, 128), (0, 512, 512, 128), (1, 0, 512, 128), (1, 512, 256, 64), (1, 768, 256, 160)]
-W_CHUNKS = [(0, 0, 64, 0), (0, 64, 64, 0), (1, 0, 64, 16), (1, 64, 64, 44)]
+X_CHUNKS = [(0, 0, 512, 128), (0, 512, 512, 128), (1, 0, 512, 128), (1, 512, 256, 64), (1, 768, 128, 64), (1, 896, 128, 96)]
+W_CHUNKS = [(0, 0, 64, 0), (0, 64, 64, 0), (1, 0, 64, 32), (1, 64, 64, 44)]
 SPANS = [(0, 384), (384, 128)]
 
 
@@ -52,15 +52,15 @@ def tile_picked_dconv_silu_e_kernel(tc, xT, w1, w2_words, w2_scales, taps, offs,
             x_raw.append(raw)
             if c == 0:
                 nc.sync.dma_start(offsets[:], offs)
-        nc.sync.dma_start(out=taps_sb[:], in_=taps.rearrange("(p t) d -> p t d", t=PACK))
         w_raw = []
         for c, (g, m0, m, mv) in enumerate(W_CHUNKS):
-            raw = keep.tile([P, PACK, PACK * m], F32, name=f"w_raw{c}")
+            raw = keep.tile([P, PACK, PACK * m], F32, name=f"w_raw{c}", tag=f"w_raw{c}", align_bytes=64)
             nc.sync.dma_start(
                 out=raw[:],
                 in_=w1[g * K_PASS : (g + 1) * K_PASS, PACK * m0 : PACK * (m0 + m)].rearrange("(p j) n -> p j n", j=PACK),
             )
             w_raw.append(raw)
+        nc.sync.dma_start(out=taps_sb[:], in_=taps.rearrange("(p t) d -> p t d", t=PACK))
         w2_codes = keep.tile([P, N], U32, name="w2_codes", align_bytes=64)
         nc.sync.dma_start(out=w2_codes[:].bitcast(I32), in_=w2_words[0].rearrange("p n r -> p (n r)").bitcast(I32))
         for q in range(4):
@@ -89,22 +89,7 @@ def tile_picked_dconv_silu_e_kernel(tc, xT, w1, w2_words, w2_scales, taps, offs,
                 nc.vector.tensor_copy(picked_words[g][:], x_words[g][:].indirect(offsets[:]))
 
         w_grouped = [keep.tile([P, PACK, P, PACK], BF16, name=f"w_grouped{g}", align_bytes=64) for g in range(PASSES)]
-        w_words = [keep.tile([P, H], U32, name=f"w_words{g}", align_bytes=64) for g in range(PASSES)]
-        w_scales = [keep.tile([P, H], U8, name=f"w_scales{g}", align_bytes=64) for g in range(PASSES)]
         banks = [psum.tile([P, S], F32, name=f"h_bank{t}") for t in range(PACK)]
-
-        def first_product(g, t):
-            cols = slice(t * P, (t + 1) * P)
-            nc.tensor.matmul_mx(
-                out=banks[t][:],
-                lhsT=w_words[g][:, cols].bitcast(FP8X4),
-                lhsT_scale=w_scales[g][:, cols],
-                rhs=picked_words[g][:].bitcast(FP8X4),
-                rhs_scale=picked_scales[4 * g :, :],
-                start=(g == 0),
-                stop=(g == PASSES - 1),
-            )
-
         for c, (g, m0, m, mv) in enumerate(W_CHUNKS):
             ms = m - mv
             dst = w_grouped[g][:, :, m0 : m0 + m, :].rearrange("p t m j -> p m j t")
@@ -112,57 +97,91 @@ def tile_picked_dconv_silu_e_kernel(tc, xT, w1, w2_words, w2_scales, taps, offs,
             nc.scalar.activation(dst[:, 0:ms], src[:, 0:ms], COPY)
             if mv:
                 nc.vector.tensor_copy(dst[:, ms:], src[:, ms:])
-            if m0 + m == P:
-                if g == 0:
-                    nc.vector.quantize_mx(
-                        out=w_words[g][:].bitcast(FP8X4),
-                        scales=w_scales[g][:],
-                        in_=w_grouped[g][:].rearrange("p t m j -> p (t m j)"),
-                    )
-                    first_product(0, 0)
-                    first_product(0, 1)
-                    first_product(0, 2)
-                else:
-                    for t in range(PACK):
-                        cols = slice(t * P, (t + 1) * P)
-                        nc.vector.quantize_mx(
-                            out=w_words[g][:, cols].bitcast(FP8X4),
-                            scales=w_scales[g][:, cols],
-                            in_=w_grouped[g][:, t].rearrange("p m j -> p (m j)"),
-                        )
+
+        w_scales = [keep.tile([P, H], U8, name=f"w_scales{g}", align_bytes=64) for g in range(PASSES)]
+        first_words = keep.tile([P, PASSES, P], U32, name="first_words", align_bytes=64)
+        later_words = keep.tile([P, PASSES, H - P], U32, name="later_words", tag=f"w_raw{len(W_CHUNKS) - 1}", align_bytes=64)
+
+        def w_words(g, t0, t1):
+            return first_words[:, g, :] if t0 == 0 else later_words[:, g, (t0 - 1) * P : (t1 - 1) * P]
+
+        def quantise_w(g, t0, t1):
+            nc.vector.quantize_mx(
+                out=w_words(g, t0, t1).bitcast(FP8X4),
+                scales=w_scales[g][:, t0 * P : t1 * P],
+                in_=w_grouped[g][:, t0:t1].rearrange("p t m j -> p (t m j)"),
+            )
+
+        def first_product(g, t):
+            nc.tensor.matmul_mx(
+                out=banks[t][:],
+                lhsT=w_words(g, t, t + 1).bitcast(FP8X4),
+                lhsT_scale=w_scales[g][:, t * P : (t + 1) * P],
+                rhs=picked_words[g][:].bitcast(FP8X4),
+                rhs_scale=picked_scales[4 * g :, :],
+                start=(g == 0),
+                stop=(g == PASSES - 1),
+            )
+
+        for t0, t1 in ((0, 1), (1, 2), (2, 4)):
+            for g in range(PASSES):
+                quantise_w(g, t0, t1)
 
         conv = [keep.tile([P, PACK, n], F32, name=f"conv{s}") for s, (n0, n) in enumerate(SPANS)]
 
-        def tap_zero(s, t):
-            n0, n = SPANS[s]
-            if t == 0:
-                nc.vector.tensor_scalar(conv[s][:, t, :], banks[t][:, n0 : n0 + n], taps_sb[:, t, 0:1], None, MULT)
-            else:
-                nc.scalar.activation(conv[s][:, t, :], banks[t][:, n0 : n0 + n], COPY, scale=taps_sb[:, t, 0:1])
+        side = [keep.tile([P, 3, n], F32, name=f"side{s}") for s, (n0, n) in enumerate(SPANS)]
 
-        def tap_add(s, t, d):
+        def acc(s, t, a):
+            return conv[s][:, t, :] if a < 0 else side[s][:, a, :]
+
+        def tap_product(s, t, d, a):
             n0, n = SPANS[s]
             skip = max(d - n0, 0)
+            src = banks[t][:, n0 + skip - d : n0 + n - d]
+            if t == 0:
+                nc.vector.tensor_scalar(acc(s, t, a)[:, skip:], src, taps_sb[:, t, d : d + 1], None, MULT)
+            else:
+                nc.scalar.activation(acc(s, t, a)[:, skip:], src, COPY, scale=taps_sb[:, t, d : d + 1])
+
+        def tap_add(s, t, d, a, lo=0, hi=None):
+            n0, n = SPANS[s]
+            hi = n if hi is None else hi
+            lo = max(lo, d - n0)
             nc.vector.scalar_tensor_tensor(
-                out=conv[s][:, t, skip:],
-                in0=banks[t][:, n0 + skip - d : n0 + n - d],
+                out=acc(s, t, a)[:, lo:hi],
+                in0=banks[t][:, n0 + lo - d : n0 + hi - d],
                 scalar=taps_sb[:, t, d : d + 1],
-                in1=conv[s][:, t, skip:],
+                in1=acc(s, t, a)[:, lo:hi],
                 op0=MULT,
                 op1=ADD,
             )
 
-        for t in range(PACK):
-            if t >= 3:
-                first_product(0, t)
-            first_product(1, t)
-            tap_zero(0, t)
-            tap_zero(1, t)
+        def join(s, t, d, a, tiles):
+            skip = max(d - SPANS[s][0], 0)
+            nc.gpsimd.tensor_tensor(
+                conv[s][:, t : t + tiles, skip:], conv[s][:, t : t + tiles, skip:], side[s][:, a : a + tiles, skip:], ADD
+            )
 
-        order = [(0, 0, 1), (1, 0, 1), (0, 0, 2), (1, 0, 2), (0, 1, 1), (0, 0, 3), (0, 1, 2), (0, 2, 1), (0, 1, 3),
-                 (0, 2, 2), (0, 3, 1), (0, 2, 3), (0, 3, 2), (1, 0, 3), (0, 3, 3)]
-        for s, t, d in order:
-            tap_add(s, t, d)
+        for t in range(PACK):
+            first_product(0, t)
+            first_product(1, t)
+            tap_product(0, t, 0, -1)
+            if t in (1, 2):
+                tap_product(0, t, 2, t - 1)
+            tap_product(1, t, 0, -1)
+            if t in (1, 2):
+                tap_product(1, t, 2, t - 1)
+
+        for d in range(1, D):
+            tap_add(0, 0, d, -1)
+            tap_add(1, 0, d, -1)
+        for t in (1, 2):
+            tap_add(0, t, 1, -1)
+            tap_add(0, t, 3, t - 1)
+            join(0, t, 2, t - 1, 1)
+        for d in range(1, D):
+            tap_add(0, 3, d, -1, 0, 256)
+            tap_add(0, 3, d, -1, 256, 384)
 
         z_grouped = [keep.tile([P, n, PACK], BF16, name=f"z_grouped{s}", align_bytes=64) for s, (n0, n) in enumerate(SPANS)]
         z_words = keep.tile([P, S], U32, name="z_words", align_bytes=64)
@@ -206,11 +225,13 @@ def tile_picked_dconv_silu_e_kernel(tc, xT, w1, w2_words, w2_scales, taps, offs,
 
         activate(0, 0, 256)
         activate(0, 256, 128)
+        for t in (1, 2):
+            tap_add(1, t, 1, -1)
+            tap_add(1, t, 3, t - 1)
+        join(1, 1, 2, 0, 2)
         for d in range(1, D):
-            for t in range(1, PACK):
-                tap_add(1, t, d)
-            if d == 2:
-                second_product(0, 0, 256)
+            tap_add(1, 3, d, -1)
+        second_product(0, 0, 256)
         activate(1, 0, 128)
         second_product(0, 256, 128)
         store(0)

@@ -91,12 +91,13 @@ def tile_picked_dconv_silu_e_kernel(tc, xT, w1, w2_words, w2_scales, taps, offs,
         w_grouped = [keep.tile([P, PACK, P, PACK], BF16, name=f"w_grouped{g}", align_bytes=64) for g in range(PASSES)]
         banks = [psum.tile([P, S], F32, name=f"h_bank{t}") for t in range(PACK)]
         for c, (g, m0, m, mv) in enumerate(W_CHUNKS):
-            ms = m - mv
             dst = w_grouped[g][:, :, m0 : m0 + m, :].rearrange("p t m j -> p m j t")
             src = w_raw[c][:].rearrange("p j (m t) -> p m j t", t=PACK)
-            nc.scalar.activation(dst[:, 0:ms], src[:, 0:ms], COPY)
-            if mv:
-                nc.vector.tensor_copy(dst[:, ms:], src[:, ms:])
+            if g == PASSES - 1:
+                nc.vector.tensor_copy(dst[:, :, :, 0:2], src[:, :, :, 0:2])
+            else:
+                nc.scalar.activation(dst[:, :, :, 0:2], src[:, :, :, 0:2], COPY)
+            nc.scalar.activation(dst[:, :, :, 2:4], src[:, :, :, 2:4], COPY)
 
         w_scales = [keep.tile([P, H], U8, name=f"w_scales{g}", align_bytes=64) for g in range(PASSES)]
         first_words = keep.tile([P, PASSES, P], U32, name="first_words", align_bytes=64)

@@ -1,6 +1,7 @@
 from contextlib import ExitStack
 
 import concourse.mybir as mybir
+from concourse.masks import make_identity
 
 K, T, S, D, H, N = 1024, 1024, 512, 4, 512, 128
 FLOPS = 2 * K * H * S + 2 * H * N * S
@@ -24,6 +25,7 @@ PASSES = K // K_PASS
 
 X_CHUNKS = [(0, 0, 512, 128), (0, 512, 512, 128), (1, 0, 512, 128), (1, 512, 256, 64), (1, 768, 128, 64), (1, 896, 128, 96)]
 W_CHUNKS = [(0, 0, 64, 0), (0, 64, 64, 0), (1, 0, 64, 32), (1, 64, 64, 44)]
+HALF = S // 2
 SPANS = [(0, 384), (384, 128)]
 
 
@@ -42,6 +44,11 @@ def tile_picked_dconv_silu_e_kernel(tc, xT, w1, w2_words, w2_scales, taps, offs,
         w2_plane = keep.tile([P, N], U8, name="w2_plane", align_bytes=64)
         nc.vector.memset(x_scales[:].bitcast(I32), 0)
         nc.vector.memset(w2_plane[:].bitcast(I32), 0)
+
+        identity = keep.tile([P, P], F32, name="identity")
+        make_identity(nc, identity[:])
+        products = [keep.tile([P, D - 1, HALF], F32, name=f"products{h}") for h in range(2)]
+        nc.vector.memset(products[0][:, :, 0:D], 0.0)
 
         offsets = keep.tile([P, S // 16], U16, name="offsets")
         taps_sb = keep.tile([P, PACK, D], F32, name="taps_sb")
@@ -91,20 +98,19 @@ def tile_picked_dconv_silu_e_kernel(tc, xT, w1, w2_words, w2_scales, taps, offs,
         w_grouped = [keep.tile([P, PACK, P, PACK], BF16, name=f"w_grouped{g}", align_bytes=64) for g in range(PASSES)]
         banks = [psum.tile([P, S], F32, name=f"h_bank{t}") for t in range(PACK)]
         for c, (g, m0, m, mv) in enumerate(W_CHUNKS):
+            ms = m - mv
             dst = w_grouped[g][:, :, m0 : m0 + m, :].rearrange("p t m j -> p m j t")
             src = w_raw[c][:].rearrange("p j (m t) -> p m j t", t=PACK)
-            if g == PASSES - 1:
-                nc.vector.tensor_copy(dst[:, :, :, 0:2], src[:, :, :, 0:2])
-            else:
-                nc.scalar.activation(dst[:, :, :, 0:2], src[:, :, :, 0:2], COPY)
-            nc.scalar.activation(dst[:, :, :, 2:4], src[:, :, :, 2:4], COPY)
+            nc.scalar.activation(dst[:, 0:ms], src[:, 0:ms], COPY)
+            if mv:
+                nc.vector.tensor_copy(dst[:, ms:], src[:, ms:])
 
         w_scales = [keep.tile([P, H], U8, name=f"w_scales{g}", align_bytes=64) for g in range(PASSES)]
-        first_words = keep.tile([P, PASSES, P], U32, name="first_words", align_bytes=64)
-        later_words = keep.tile([P, PASSES, H - P], U32, name="later_words", tag=f"w_raw{len(W_CHUNKS) - 1}", align_bytes=64)
+        first_words = keep.tile([P, PASSES, 2 * P], U32, name="first_words", align_bytes=64)
+        later_words = keep.tile([P, PASSES, 2 * P], U32, name="later_words", tag=f"w_raw{len(W_CHUNKS) - 1}", align_bytes=64)
 
         def w_words(g, t0, t1):
-            return first_words[:, g, :] if t0 == 0 else later_words[:, g, (t0 - 1) * P : (t1 - 1) * P]
+            return first_words[:, g, t0 * P : t1 * P] if t0 < 2 else later_words[:, g, (t0 - 2) * P : (t1 - 2) * P]
 
         def quantise_w(g, t0, t1):
             nc.vector.quantize_mx(
@@ -124,70 +130,94 @@ def tile_picked_dconv_silu_e_kernel(tc, xT, w1, w2_words, w2_scales, taps, offs,
                 stop=(g == PASSES - 1),
             )
 
-        for t0, t1 in ((0, 1), (1, 2), (2, 4)):
-            for g in range(PASSES):
-                quantise_w(g, t0, t1)
+        quantise_w(0, 0, 2)
+        quantise_w(1, 0, 1)
+        quantise_w(1, 1, 2)
+        quantise_w(0, 2, 4)
+        quantise_w(1, 2, 4)
 
         conv = [keep.tile([P, PACK, n], F32, name=f"conv{s}") for s, (n0, n) in enumerate(SPANS)]
 
-        side = [keep.tile([P, 3, n], F32, name=f"side{s}") for s, (n0, n) in enumerate(SPANS)]
+        def tap_zero(s, t):
+            n0, n = SPANS[s]
+            if t == 0:
+                nc.vector.tensor_scalar(conv[s][:, t, :], banks[t][:, n0 : n0 + n], taps_sb[:, t, 0:1], None, MULT)
+            else:
+                nc.scalar.activation(conv[s][:, t, :], banks[t][:, n0 : n0 + n], COPY, scale=taps_sb[:, t, 0:1])
 
-        def acc(s, t, a):
-            return conv[s][:, t, :] if a < 0 else side[s][:, a, :]
-
-        def tap_product(s, t, d, a):
+        def tap_add(s, t, d):
             n0, n = SPANS[s]
             skip = max(d - n0, 0)
-            src = banks[t][:, n0 + skip - d : n0 + n - d]
-            if t == 0:
-                nc.vector.tensor_scalar(acc(s, t, a)[:, skip:], src, taps_sb[:, t, d : d + 1], None, MULT)
-            else:
-                nc.scalar.activation(acc(s, t, a)[:, skip:], src, COPY, scale=taps_sb[:, t, d : d + 1])
-
-        def tap_add(s, t, d, a, lo=0, hi=None):
-            n0, n = SPANS[s]
-            hi = n if hi is None else hi
-            lo = max(lo, d - n0)
             nc.vector.scalar_tensor_tensor(
-                out=acc(s, t, a)[:, lo:hi],
-                in0=banks[t][:, n0 + lo - d : n0 + hi - d],
+                out=conv[s][:, t, skip:],
+                in0=banks[t][:, n0 + skip - d : n0 + n - d],
                 scalar=taps_sb[:, t, d : d + 1],
-                in1=acc(s, t, a)[:, lo:hi],
+                in1=conv[s][:, t, skip:],
                 op0=MULT,
                 op1=ADD,
             )
 
-        def join(s, t, d, a, tiles):
-            skip = max(d - SPANS[s][0], 0)
-            nc.gpsimd.tensor_tensor(
-                conv[s][:, t : t + tiles, skip:], conv[s][:, t : t + tiles, skip:], side[s][:, a : a + tiles, skip:], ADD
-            )
+        turned_banks = [psum.tile([P, 2, P], F32, name=f"turned_bank{h}", tag=f"turned_bank{h}") for h in range(2)]
+        back_banks = [psum.tile([P, HALF], F32, name=f"back_bank{h}") for h in range(2)]
+        turned = [keep.tile([P, 2, P], F32, name=f"turned{h}") for h in range(2)]
 
-        for t in range(PACK):
+        def sum_on_tensor(t, h):
+            n0 = h * HALF
+            for d in range(1, D):
+                skip = max(d - n0, 0)
+                nc.scalar.activation(
+                    products[h][:, d - 1, skip:], banks[t][:, n0 + skip - d : n0 + HALF - d], COPY, scale=taps_sb[:, t, d : d + 1]
+                )
+            for b in range(2):
+                for d in range(1, D):
+                    nc.tensor.matmul(
+                        turned_banks[h][:, b, :],
+                        lhsT=products[h][:, d - 1, b * P : (b + 1) * P],
+                        rhs=identity[:],
+                        is_transpose=True,
+                        start=(d == 1),
+                        stop=(d == D - 1),
+                    )
+
+        def turn_back(t, h):
+            nc.scalar.copy(turned[h][:], turned_banks[h][:])
+            for b in range(2):
+                nc.tensor.transpose(back_banks[h][:, b * P : (b + 1) * P], turned[h][:, b, :], identity[:])
+
+        def add_back(dst, src):
+            nc.vector.tensor_tensor(dst, src, dst, ADD)
+
+        first_product(0, 0)
+        first_product(0, 1)
+        first_product(1, 0)
+        first_product(1, 1)
+        for t in (2, 3):
             first_product(0, t)
             first_product(1, t)
-            tap_product(0, t, 0, -1)
-            if t in (1, 2):
-                tap_product(0, t, 2, t - 1)
-            tap_product(1, t, 0, -1)
-            if t in (1, 2):
-                tap_product(1, t, 2, t - 1)
-
+        tap_zero(0, 0)
+        tap_zero(1, 0)
+        sum_on_tensor(1, 0)
+        for t in (2, 3):
+            tap_zero(0, t)
+            tap_zero(1, t)
+        sum_on_tensor(1, 1)
+        turn_back(1, 0)
+        turn_back(1, 1)
+        tap_zero(0, 1)
+        tap_zero(1, 1)
         for d in range(1, D):
-            tap_add(0, 0, d, -1)
-            tap_add(1, 0, d, -1)
-        for t in (1, 2):
-            tap_add(0, t, 1, -1)
-            tap_add(0, t, 3, t - 1)
-            join(0, t, 2, t - 1, 1)
+            tap_add(0, 0, d)
+            tap_add(1, 0, d)
         for d in range(1, D):
-            tap_add(0, 3, d, -1, 0, 256)
-            tap_add(0, 3, d, -1, 256, 384)
+            tap_add(0, 2, d)
+            tap_add(0, 3, d)
+        add_back(conv[0][:, 1, 0:HALF], back_banks[0][:])
+        add_back(conv[0][:, 1, HALF:], back_banks[1][:, 0:P])
 
         z_grouped = [keep.tile([P, n, PACK], BF16, name=f"z_grouped{s}", align_bytes=64) for s, (n0, n) in enumerate(SPANS)]
         z_words = keep.tile([P, S], U32, name="z_words", align_bytes=64)
         z_scales = keep.tile([P, S], U8, name="z_scales", align_bytes=64)
-        out_banks = [psum.tile([P, n], F32, name=f"out_bank{s}") for s, (n0, n) in enumerate(SPANS)]
+        out_banks = [psum.tile([P, n], F32, name=f"out_bank{s}", tag=f"turned_bank{s}") for s, (n0, n) in enumerate(SPANS)]
         staged = [keep.tile([P, n], F32, name=f"staged{s}") for s, (n0, n) in enumerate(SPANS)]
 
         def activate(s, a, n):
@@ -226,12 +256,10 @@ def tile_picked_dconv_silu_e_kernel(tc, xT, w1, w2_words, w2_scales, taps, offs,
 
         activate(0, 0, 256)
         activate(0, 256, 128)
-        for t in (1, 2):
-            tap_add(1, t, 1, -1)
-            tap_add(1, t, 3, t - 1)
-        join(1, 1, 2, 0, 2)
         for d in range(1, D):
-            tap_add(1, 3, d, -1)
+            for t in (2, 3):
+                tap_add(1, t, d)
+        add_back(conv[1][:, 1, :], back_banks[1][:, P:])
         second_product(0, 0, 256)
         activate(1, 0, 128)
         second_product(0, 256, 128)

from contextlib import ExitStack

import concourse.mybir as mybir
from concourse.masks import make_identity

K, T, S, D, H, N = 1024, 1024, 512, 4, 512, 128
FLOPS = 2 * K * H * S + 2 * H * N * S

F32 = mybir.dt.float32
BF16 = mybir.dt.bfloat16
I32 = mybir.dt.int32
U32 = mybir.dt.uint32
U16 = mybir.dt.uint16
U8 = mybir.dt.uint8
FP8X4 = mybir.dt.float8_e4m3fn_x4
COPY = mybir.ActivationFunctionType.Copy
SILU = mybir.ActivationFunctionType.Silu
MULT = mybir.AluOpType.mult
ADD = mybir.AluOpType.add

P = 128
PACK = 4
K_PASS = P * PACK
PASSES = K // K_PASS

X_CHUNKS = [(0, 0, 512, 128), (0, 512, 512, 128), (1, 0, 512, 128), (1, 512, 256, 64), (1, 768, 128, 64), (1, 896, 128, 96)]
W_CHUNKS = [(0, 0, 64, 0), (0, 64, 64, 0), (1, 0, 64, 32), (1, 64, 64, 44)]
HALF = S // 2
SPANS = [(0, 384), (384, 128)]


def tile_picked_dconv_silu_e_kernel(tc, xT, w1, w2_words, w2_scales, taps, offs, out):
    nc = tc.nc
    with ExitStack() as ctx:
        keep = ctx.enter_context(tc.tile_pool(name="keep", bufs=1))
        psum = ctx.enter_context(tc.psum_pool(name="psum", bufs=1))

        zero_in = keep.tile([P, 1], F32, name="zero_in")
        zero_bias = keep.tile([P, 1], F32, name="zero_bias")
        nc.vector.memset(zero_in[:], 0.0)
        nc.scalar.activation(zero_bias[:], zero_in[:], SILU)

        x_scales = keep.tile([P, T], U8, name="x_scales", align_bytes=64)
        w2_plane = keep.tile([P, N], U8, name="w2_plane", align_bytes=64)
        nc.vector.memset(x_scales[:].bitcast(I32), 0)
        nc.vector.memset(w2_plane[:].bitcast(I32), 0)

        identity = keep.tile([P, P], F32, name="identity")
        make_identity(nc, identity[:])
        products = [keep.tile([P, D - 1, HALF], F32, name=f"products{h}") for h in range(2)]
        nc.vector.memset(products[0][:, :, 0:D], 0.0)

        offsets = keep.tile([P, S // 16], U16, name="offsets")
        taps_sb = keep.tile([P, PACK, D], F32, name="taps_sb")
        x_raw = []
        for c, (g, n0, n, nv) in enumerate(X_CHUNKS):
            raw = keep.tile([P, PACK, n], F32, name=f"x_raw{c}")
            nc.sync.dma_start(out=raw[:], in_=xT[g * K_PASS : (g + 1) * K_PASS, n0 : n0 + n].rearrange("(p j) n -> p j n", j=PACK))
            x_raw.append(raw)
            if c == 0:
                nc.sync.dma_start(offsets[:], offs)
        w_raw = []
        for c, (g, m0, m, mv) in enumerate(W_CHUNKS):
            raw = keep.tile([P, PACK, PACK * m], F32, name=f"w_raw{c}", tag=f"w_raw{c}", align_bytes=64)
            nc.sync.dma_start(
                out=raw[:],
                in_=w1[g * K_PASS : (g + 1) * K_PASS, PACK * m0 : PACK * (m0 + m)].rearrange("(p j) n -> p j n", j=PACK),
            )
            w_raw.append(raw)
        nc.sync.dma_start(out=taps_sb[:], in_=taps.rearrange("(p t) d -> p t d", t=PACK))
        w2_codes = keep.tile([P, N], U32, name="w2_codes", align_bytes=64)
        nc.sync.dma_start(out=w2_codes[:].bitcast(I32), in_=w2_words[0].rearrange("p n r -> p (n r)").bitcast(I32))
        for q in range(4):
            nc.sync.dma_start(
                out=w2_plane[32 * q : 32 * q + 4, :].bitcast(I32), in_=w2_scales[0, 4 * q : 4 * q + 4, :].bitcast(I32)
            )

        x_words = [keep.tile([P, T], U32, name=f"x_words{g}", align_bytes=64) for g in range(PASSES)]
        picked_words = [keep.tile([P, S], U32, name=f"picked_words{g}", align_bytes=64) for g in range(PASSES)]
        picked_scales = keep.tile([P, S], U8, name="picked_scales", align_bytes=64)
        for c, (g, n0, n, nv) in enumerate(X_CHUNKS):
            grouped = keep.tile([P, n, PACK], BF16, name=f"x_grouped{c}", align_bytes=64)
            ns = n - nv
            dst = grouped[:].rearrange("p (c i) j -> p c j i", i=4)
            src = x_raw[c][:].rearrange("p j (c i) -> p c j i", i=4)
            nc.scalar.activation(dst[:, 0 : ns // 4], src[:, 0 : ns // 4], COPY)
            nc.vector.tensor_copy(dst[:, ns // 4 :], src[:, ns // 4 :])
            nc.vector.quantize_mx(
                out=x_words[g][:, n0 : n0 + n].bitcast(FP8X4),
                scales=x_scales[4 * g :, n0 : n0 + n],
                in_=grouped[:].rearrange("p n j -> p (n j)"),
            )
            if n0 + n == T:
                if g == PASSES - 1:
                    nc.vector.tensor_copy(picked_scales[:], x_scales[:].indirect(offsets[:]))
                nc.vector.tensor_copy(picked_words[g][:], x_words[g][:].indirect(offsets[:]))

        w_grouped = [keep.tile([P, PACK, P, PACK], BF16, name=f"w_grouped{g}", align_bytes=64) for g in range(PASSES)]
        banks = [psum.tile([P, S], F32, name=f"h_bank{t}") for t in range(PACK)]
        for c, (g, m0, m, mv) in enumerate(W_CHUNKS):
            ms = m - mv
            dst = w_grouped[g][:, :, m0 : m0 + m, :].rearrange("p t m j -> p m j t")
            src = w_raw[c][:].rearrange("p j (m t) -> p m j t", t=PACK)
            nc.scalar.activation(dst[:, 0:ms], src[:, 0:ms], COPY)
            if mv:
                nc.vector.tensor_copy(dst[:, ms:], src[:, ms:])

        w_scales = [keep.tile([P, H], U8, name=f"w_scales{g}", align_bytes=64) for g in range(PASSES)]
        first_words = keep.tile([P, PASSES, 2 * P], U32, name="first_words", align_bytes=64)
        later_words = keep.tile([P, PASSES, 2 * P], U32, name="later_words", tag=f"w_raw{len(W_CHUNKS) - 1}", align_bytes=64)

        def w_words(g, t0, t1):
            return first_words[:, g, t0 * P : t1 * P] if t0 < 2 else later_words[:, g, (t0 - 2) * P : (t1 - 2) * P]

        def quantise_w(g, t0, t1):
            nc.vector.quantize_mx(
                out=w_words(g, t0, t1).bitcast(FP8X4),
                scales=w_scales[g][:, t0 * P : t1 * P],
                in_=w_grouped[g][:, t0:t1].rearrange("p t m j -> p (t m j)"),
            )

        def first_product(g, t):
            nc.tensor.matmul_mx(
                out=banks[t][:],
                lhsT=w_words(g, t, t + 1).bitcast(FP8X4),
                lhsT_scale=w_scales[g][:, t * P : (t + 1) * P],
                rhs=picked_words[g][:].bitcast(FP8X4),
                rhs_scale=picked_scales[4 * g :, :],
                start=(g == 0),
                stop=(g == PASSES - 1),
            )

        quantise_w(0, 0, 2)
        quantise_w(1, 0, 1)
        quantise_w(1, 1, 2)
        quantise_w(0, 2, 4)
        quantise_w(1, 2, 4)

        conv = [keep.tile([P, PACK, n], F32, name=f"conv{s}") for s, (n0, n) in enumerate(SPANS)]

        def tap_zero(s, t):
            n0, n = SPANS[s]
            if t == 0:
                nc.vector.tensor_scalar(conv[s][:, t, :], banks[t][:, n0 : n0 + n], taps_sb[:, t, 0:1], None, MULT)
            else:
                nc.scalar.activation(conv[s][:, t, :], banks[t][:, n0 : n0 + n], COPY, scale=taps_sb[:, t, 0:1])

        def tap_add(s, t, d):
            n0, n = SPANS[s]
            skip = max(d - n0, 0)
            nc.vector.scalar_tensor_tensor(
                out=conv[s][:, t, skip:],
                in0=banks[t][:, n0 + skip - d : n0 + n - d],
                scalar=taps_sb[:, t, d : d + 1],
                in1=conv[s][:, t, skip:],
                op0=MULT,
                op1=ADD,
            )

        turned_banks = [psum.tile([P, 2, P], F32, name=f"turned_bank{h}", tag=f"turned_bank{h}") for h in range(2)]
        back_banks = [psum.tile([P, HALF], F32, name=f"back_bank{h}") for h in range(2)]
        turned = [keep.tile([P, 2, P], F32, name=f"turned{h}") for h in range(2)]

        def sum_on_tensor(t, h):
            n0 = h * HALF
            for d in range(1, D):
                skip = max(d - n0, 0)
                nc.scalar.activation(
                    products[h][:, d - 1, skip:], banks[t][:, n0 + skip - d : n0 + HALF - d], COPY, scale=taps_sb[:, t, d : d + 1]
                )
            for b in range(2):
                for d in range(1, D):
                    nc.tensor.matmul(
                        turned_banks[h][:, b, :],
                        lhsT=products[h][:, d - 1, b * P : (b + 1) * P],
                        rhs=identity[:],
                        is_transpose=True,
                        start=(d == 1),
                        stop=(d == D - 1),
                    )

        def turn_back(t, h):
            nc.scalar.copy(turned[h][:], turned_banks[h][:])
            for b in range(2):
                nc.tensor.transpose(back_banks[h][:, b * P : (b + 1) * P], turned[h][:, b, :], identity[:])

        def add_back(dst, src):
            nc.vector.tensor_tensor(dst, src, dst, ADD)

        first_product(0, 0)
        first_product(0, 1)
        first_product(1, 0)
        first_product(1, 1)
        for t in (2, 3):
            first_product(0, t)
            first_product(1, t)
        tap_zero(0, 0)
        tap_zero(1, 0)
        sum_on_tensor(1, 0)
        for t in (2, 3):
            tap_zero(0, t)
            tap_zero(1, t)
        sum_on_tensor(1, 1)
        turn_back(1, 0)
        turn_back(1, 1)
        tap_zero(0, 1)
        tap_zero(1, 1)
        for d in range(1, D):
            tap_add(0, 0, d)
            tap_add(1, 0, d)
        for d in range(1, D):
            tap_add(0, 2, d)
            tap_add(0, 3, d)
        add_back(conv[0][:, 1, 0:HALF], back_banks[0][:])
        add_back(conv[0][:, 1, HALF:], back_banks[1][:, 0:P])

        z_grouped = [keep.tile([P, n, PACK], BF16, name=f"z_grouped{s}", align_bytes=64) for s, (n0, n) in enumerate(SPANS)]
        z_words = keep.tile([P, S], U32, name="z_words", align_bytes=64)
        z_scales = keep.tile([P, S], U8, name="z_scales", align_bytes=64)
        out_banks = [psum.tile([P, n], F32, name=f"out_bank{s}", tag=f"turned_bank{s}") for s, (n0, n) in enumerate(SPANS)]
        staged = [keep.tile([P, n], F32, name=f"staged{s}") for s, (n0, n) in enumerate(SPANS)]

        def activate(s, a, n):
            nc.scalar.activation(
                z_grouped[s][:, a : a + n, :].rearrange("p (c i) t -> p c t i", i=4),
                conv[s][:, :, a : a + n].rearrange("p t (c i) -> p c t i", i=4),
                SILU,
                bias=zero_bias[:],
            )

        def second_product(s, a, n):
            n0 = SPANS[s][0]
            cols = slice(n0 + a, n0 + a + n)
            nc.vector.quantize_mx(
                out=z_words[:, cols].bitcast(FP8X4),
                scales=z_scales[:, cols],
                in_=z_grouped[s][:, a : a + n, :].rearrange("p n t -> p (n t)"),
            )
            nc.tensor.matmul_mx(
                out=out_banks[s][:, a : a + n],
                lhsT=w2_codes[:].bitcast(FP8X4),
                lhsT_scale=w2_plane[:],
                rhs=z_words[:, cols].bitcast(FP8X4),
                rhs_scale=z_scales[:, cols],
                start=True,
                stop=True,
            )

        def store(s):
            n0, n = SPANS[s]
            if s == 0:
                nc.scalar.copy(staged[s][:], out_banks[s][:])
            else:
                nc.vector.tensor_copy(staged[s][:], out_banks[s][:])
            nc.sync.dma_start(out=out[:, n0 : n0 + n], in_=staged[s][:])

        activate(0, 0, 256)
        activate(0, 256, 128)
        for d in range(1, D):
            for t in (2, 3):
                tap_add(1, t, d)
        add_back(conv[1][:, 1, :], back_banks[1][:, P:])
        second_product(0, 0, 256)
        activate(1, 0, 128)
        second_product(0, 256, 128)
        store(0)
        second_product(1, 0, 128)
        store(1)
